import numpy as np, ml_dtypes
CORES = [6,14,30,38,62,70,86,94,102]
N = 9
KT, C = 4, 64
B = 2
def setup_inputs(rng):
    return {"x": rng.standard_normal((N, 128, KT * C), dtype=np.float32).astype(ml_dtypes.bfloat16)}
def setup_inputs_big(rng):
    d = setup_inputs(rng)
    for k in ("x",): d[k] = (d[k].astype(np.float32) * 1024.0).astype(d[k].dtype)
    return d
def setup_inputs_small(rng):
    d = setup_inputs(rng)
    for k in ("x",): d[k] = (d[k].astype(np.float32) * (1 / 1024.0)).astype(d[k].dtype)
    return d
def setup_inputs_apart(rng):
    d = setup_inputs(rng)
    f = (10.0 ** rng.permutation(np.linspace(-1.5, 1.5, N))).astype(np.float32).reshape(N, 1, 1)
    for k in ("x",): d[k] = (d[k].astype(np.float32) * f).astype(d[k].dtype)
    return d
def reference(x):
    X = x.astype(np.float64)
    y = np.full((N, C, (2 * B + 1) * C), np.nan)
    for r in range(N):
        for i in range(2 * B + 1):
            s = (r + i - B) % N
            if s != r: y[r][:, C * i:C * i + C] = sum(X[r][:, C * t:C * t + C].T @ X[s][:, C * t:C * t + C] for t in range(KT))
    return {"y": y.astype(ml_dtypes.bfloat16 if x.dtype != np.float64 else np.float64)}

@@ -1,0 +1,74 @@
+from concourse.bass import DstId, RemoteDMATransfer
+
+KT, C, B = 4, 64, 2
+W = KT * C
+OFFS = [k for k in range(-B, B + 1) if k != 0]
+
+SCRATCH = {
+    "xs": ("sbuf", [128, W], "bfloat16"),
+    "land": ("sbuf", [128, len(OFFS) * W], "bfloat16"),
+    "out": ("sbuf", [128, (2 * B + 1) * C], "bfloat16"),
+    "ps0": ("psum", [128, 512], "float32"),
+    "ps1": ("psum", [128, 512], "float32"),
+    "ps2": ("psum", [128, 512], "float32"),
+    "ps3": ("psum", [128, 512], "float32"),
+}
+SEMAPHORES = ["loaded", "sent", "arr0", "arr1", "arr2", "arr3", "mm0", "mm1", "mm2", "mm3", "cp", "stored"]
+
+
+def engines_of(mask):
+    return [e for e in range(16) if (mask >> e) & 1]
+
+
+def mask_of(engines):
+    m = 0
+    for e in engines:
+        m |= 1 << e
+    return m
+
+
+def rank_program(g, core, T, topo):
+    rank = T.rank_of(core)
+    if rank is None:
+        return
+    n = len(T.cores)
+
+    g.sync.dma_start(T.xs[:, :], T.x[:, :]).then_inc(T.sem.loaded, 16)
+    g.vector.memset(T.out[0:C, B * C:(B + 1) * C], 0.0).then_inc(T.sem.cp, 1)
+
+    dests = [T.cores[(rank + k) % n] for k in OFFS]
+    common = 0xFFFF
+    for d in dests:
+        if not topo.may_write(core, d):
+            raise ValueError("core %d may not write to core %d" % (core, d))
+        common &= topo.mask(core, d)
+    eng = engines_of(common)
+    share = len(eng) // len(dests)
+    transfers = []
+    for i, (k, d) in enumerate(zip(OFFS, dests)):
+        rid, pid, _ = topo.addr(d)
+        j = OFFS.index(-k)
+        transfers.append(RemoteDMATransfer(
+            dst_ids=[DstId(rid=rid, pnc=pid)],
+            dma_engine_mask=mask_of(eng[i * share:(i + 1) * share]),
+            remote_sem=T.sem["arr%d" % j],
+            src=T.xs[:, :],
+            dst=T.land[:, j * W:(j + 1) * W]))
+    g.wait_ge(T.sem.loaded, 16)
+    g.remote_dma_fused(transfers, local_sem=T.sem.sent)
+
+    g.tensor.wait_ge(T.sem.loaded, 16)
+    for j, k in enumerate(OFFS):
+        ps = T["ps%d" % j]
+        g.tensor.wait_ge(T.sem["arr%d" % j], share)
+        for t in range(KT):
+            mm = g.tensor.matmul(ps[0:C, 0:C], T.xs[:, t * C:(t + 1) * C],
+                                 T.land[:, j * W + t * C:j * W + (t + 1) * C], t == 0, t == KT - 1)
+        mm.then_inc(T.sem["mm%d" % j], 1)
+        g.vector.wait_ge(T.sem["mm%d" % j], 1)
+        g.vector.tensor_copy(T.out[0:C, (k + B) * C:(k + B + 1) * C], ps[0:C, 0:C]).then_inc(T.sem.cp, 1)
+
+    g.sync.wait_ge(T.sem.cp, len(OFFS) + 1)
+    g.sync.dma_start(T.y[:, :], T.out[0:C, :]).then_inc(T.sem.stored, 16)
+    g.sync.wait_ge(T.sem.stored, 16)
+    g.wait_ge(T.sem.sent, share * len(dests))

@@ -1,12 +1,10 @@
-from concourse.bass import DstId, RemoteDMATransfer
-
 KT, C, B = 4, 64, 2
 W = KT * C
-OFFS = [k for k in range(-B, B + 1) if k != 0]
+SEND = [2, -2, 1, -1]
 
 SCRATCH = {
     "xs": ("sbuf", [128, W], "bfloat16"),
-    "land": ("sbuf", [128, len(OFFS) * W], "bfloat16"),
+    "land": ("sbuf", [128, len(SEND) * W], "bfloat16"),
     "out": ("sbuf", [128, (2 * B + 1) * C], "bfloat16"),
     "ps0": ("psum", [128, 512], "float32"),
     "ps1": ("psum", [128, 512], "float32"),
@@ -16,15 +14,13 @@ SCRATCH = {
 SEMAPHORES = ["loaded", "sent", "arr0", "arr1", "arr2", "arr3", "mm0", "mm1", "mm2", "mm3", "cp", "stored"]
 
 
-def engines_of(mask):
-    return [e for e in range(16) if (mask >> e) & 1]
-
-
-def mask_of(engines):
+def half_mask(mask, which):
+    eng = [e for e in range(16) if (mask >> e) & 1]
+    h = len(eng) // 2
     m = 0
-    for e in engines:
+    for e in eng[which * h:(which + 1) * h]:
         m |= 1 << e
-    return m
+    return m, h
 
 
 def rank_program(g, core, T, topo):
@@ -36,39 +32,32 @@ def rank_program(g, core, T, topo):
     g.sync.dma_start(T.xs[:, :], T.x[:, :]).then_inc(T.sem.loaded, 16)
     g.vector.memset(T.out[0:C, B * C:(B + 1) * C], 0.0).then_inc(T.sem.cp, 1)
 
-    dests = [T.cores[(rank + k) % n] for k in OFFS]
-    common = 0xFFFF
-    for d in dests:
+    g.wait_ge(T.sem.loaded, 16)
+    left = 0
+    for p, k in enumerate(SEND):
+        d = T.cores[(rank + k) % n]
         if not topo.may_write(core, d):
             raise ValueError("core %d may not write to core %d" % (core, d))
-        common &= topo.mask(core, d)
-    eng = engines_of(common)
-    share = len(eng) // len(dests)
-    transfers = []
-    for i, (k, d) in enumerate(zip(OFFS, dests)):
         rid, pid, _ = topo.addr(d)
-        j = OFFS.index(-k)
-        transfers.append(RemoteDMATransfer(
-            dst_ids=[DstId(rid=rid, pnc=pid)],
-            dma_engine_mask=mask_of(eng[i * share:(i + 1) * share]),
-            remote_sem=T.sem["arr%d" % j],
-            src=T.xs[:, :],
-            dst=T.land[:, j * W:(j + 1) * W]))
-    g.wait_ge(T.sem.loaded, 16)
-    g.remote_dma_fused(transfers, local_sem=T.sem.sent)
+        m, cnt = half_mask(topo.mask(core, d), p % 2)
+        g.remote_dma(out_ap=T.land[:, p * W:(p + 1) * W], in_ap=T.xs[:, :], remote_sem=T.sem["arr%d" % p],
+                     local_sem=T.sem.sent, pid=pid, routing_id=rid, dma_engine_mask=m)
+        left += cnt
 
     g.tensor.wait_ge(T.sem.loaded, 16)
-    for j, k in enumerate(OFFS):
-        ps = T["ps%d" % j]
-        g.tensor.wait_ge(T.sem["arr%d" % j], share)
+    for p, k in enumerate(SEND):
+        ps = T["ps%d" % p]
+        blk = B - k
+        _, cnt = half_mask(topo.mask(T.cores[(rank - k) % n], core), p % 2)
+        g.tensor.wait_ge(T.sem["arr%d" % p], cnt)
         for t in range(KT):
             mm = g.tensor.matmul(ps[0:C, 0:C], T.xs[:, t * C:(t + 1) * C],
-                                 T.land[:, j * W + t * C:j * W + (t + 1) * C], t == 0, t == KT - 1)
-        mm.then_inc(T.sem["mm%d" % j], 1)
-        g.vector.wait_ge(T.sem["mm%d" % j], 1)
-        g.vector.tensor_copy(T.out[0:C, (k + B) * C:(k + B + 1) * C], ps[0:C, 0:C]).then_inc(T.sem.cp, 1)
+                                 T.land[:, p * W + t * C:p * W + (t + 1) * C], t == 0, t == KT - 1)
+        mm.then_inc(T.sem["mm%d" % p], 1)
+        g.vector.wait_ge(T.sem["mm%d" % p], 1)
+        g.vector.tensor_copy(T.out[0:C, blk * C:(blk + 1) * C], ps[0:C, 0:C]).then_inc(T.sem.cp, 1)
 
-    g.sync.wait_ge(T.sem.cp, len(OFFS) + 1)
+    g.sync.wait_ge(T.sem.cp, len(SEND) + 1)
     g.sync.dma_start(T.y[:, :], T.out[0:C, :]).then_inc(T.sem.stored, 16)
     g.sync.wait_ge(T.sem.stored, 16)
-    g.wait_ge(T.sem.sent, share * len(dests))
+    g.wait_ge(T.sem.sent, left)

KT, C, B = 4, 64, 2
W = KT * C
SEND = [2, -2, 1, -1]

SCRATCH = {
    "xs": ("sbuf", [128, W], "bfloat16"),
    "land": ("sbuf", [128, len(SEND) * W], "bfloat16"),
    "out": ("sbuf", [128, (2 * B + 1) * C], "bfloat16"),
    "ps0": ("psum", [128, 512], "float32"),
    "ps1": ("psum", [128, 512], "float32"),
    "ps2": ("psum", [128, 512], "float32"),
    "ps3": ("psum", [128, 512], "float32"),
}
SEMAPHORES = ["loaded", "sent", "arr0", "arr1", "arr2", "arr3", "mm0", "mm1", "mm2", "mm3", "cp", "stored"]


def half_mask(mask, which):
    eng = [e for e in range(16) if (mask >> e) & 1]
    h = len(eng) // 2
    m = 0
    for e in eng[which * h:(which + 1) * h]:
        m |= 1 << e
    return m, h


def rank_program(g, core, T, topo):
    rank = T.rank_of(core)
    if rank is None:
        return
    n = len(T.cores)

    g.sync.dma_start(T.xs[:, :], T.x[:, :]).then_inc(T.sem.loaded, 16)
    g.vector.memset(T.out[0:C, B * C:(B + 1) * C], 0.0).then_inc(T.sem.cp, 1)

    g.wait_ge(T.sem.loaded, 16)
    left = 0
    for p, k in enumerate(SEND):
        d = T.cores[(rank + k) % n]
        if not topo.may_write(core, d):
            raise ValueError("core %d may not write to core %d" % (core, d))
        rid, pid, _ = topo.addr(d)
        m, cnt = half_mask(topo.mask(core, d), p % 2)
        g.remote_dma(out_ap=T.land[:, p * W:(p + 1) * W], in_ap=T.xs[:, :], remote_sem=T.sem["arr%d" % p],
                     local_sem=T.sem.sent, pid=pid, routing_id=rid, dma_engine_mask=m)
        left += cnt

    g.tensor.wait_ge(T.sem.loaded, 16)
    for p, k in enumerate(SEND):
        ps = T["ps%d" % p]
        blk = B - k
        _, cnt = half_mask(topo.mask(T.cores[(rank - k) % n], core), p % 2)
        g.tensor.wait_ge(T.sem["arr%d" % p], cnt)
        for t in range(KT):
            mm = g.tensor.matmul(ps[0:C, 0:C], T.xs[:, t * C:(t + 1) * C],
                                 T.land[:, p * W + t * C:p * W + (t + 1) * C], t == 0, t == KT - 1)
        mm.then_inc(T.sem["mm%d" % p], 1)
        g.vector.wait_ge(T.sem["mm%d" % p], 1)
        g.vector.tensor_copy(T.out[0:C, blk * C:(blk + 1) * C], ps[0:C, 0:C]).then_inc(T.sem.cp, 1)

    g.sync.wait_ge(T.sem.cp, len(SEND) + 1)
    g.sync.dma_start(T.y[:, :], T.out[0:C, :]).then_inc(T.sem.stored, 16)
    g.sync.wait_ge(T.sem.stored, 16)
    g.wait_ge(T.sem.sent, left)
